import numpy as np
import ml_dtypes


def mxq(x, axis, fmt="e4m3"):
    dtype, down = {"e4m3": (ml_dtypes.float8_e4m3fn, 7), "e5m2": (ml_dtypes.float8_e5m2, 14)}[fmt]
    v = np.moveaxis(np.asarray(x, np.float32).astype(ml_dtypes.bfloat16).astype(np.float64), axis, -1)
    blocks = v.reshape(v.shape[:-1] + (-1, 32))
    amax = np.abs(blocks).max(-1, keepdims=True)
    byte = np.maximum(np.where(amax > 0, np.frexp(amax)[1] - 1 + 127, 0) - down, 1)
    scale = np.exp2(byte - 127.0)
    codes = (blocks / scale).astype(np.float32).astype(dtype).astype(np.float64)
    return np.moveaxis((codes * scale).reshape(v.shape), -1, axis)


WIDE = False


def mx_kscale(k):
    if not WIDE:
        return np.ones(k)
    levels = np.array([10, -10, 5, -5, 0])
    if k % 512:
        return np.exp2(np.random.permutation(np.resize(levels, k // 32))).repeat(32)
    a = np.empty((k // 512, 16))
    for p in range(k // 512):
        a[p, :8] = np.random.permutation(np.resize(levels, 8))
        for g in range(8):
            far = levels[np.abs(levels - a[p, g]) >= 10]
            a[p, g + 8] = far[np.random.randint(len(far))]
    return np.exp2(a.ravel()).repeat(32)


def f64(x):
    return np.asarray(x).astype(np.float64)


def striped(idx):
    return np.tile(idx.reshape(-1, 16).T, (8, 1)).astype(np.uint16)


def unstriped(offs):
    return offs[:16].T.reshape(-1).astype(np.int64)


E2M1 = np.array([0.0, 0.5, 1.0, 1.5, 2.0, 3.0, 4.0, 6.0, -0.0, -0.5, -1.0, -1.5, -2.0, -3.0, -4.0, -6.0])


def pack_weight(w, fmt):
    k, n = w.shape
    w = f64(np.asarray(w, np.float32).astype(ml_dtypes.bfloat16)).reshape(k // 32, 32, n)
    amax = np.abs(w).max(1)
    if fmt == "e4m3":
        byte = np.frexp(amax)[1] - 1 + 127 - 7
    else:
        mant, ex = np.frexp(amax / 6.0)
        byte = np.where(mant > 0.5, ex, ex - 1) + 127
    byte = np.clip(np.where(amax > 0, byte, 1), 1, 254)
    scaled = (w * np.exp2(127.0 - byte)[:, None, :]).reshape(k, n).astype(np.float32)
    by_word = np.ascontiguousarray(scaled.reshape(k // 512, 128, 4, n).transpose(0, 1, 3, 2))
    if fmt == "e4m3":
        words = by_word.astype(ml_dtypes.float8_e4m3fn).view(np.uint8)
    else:
        c = by_word.astype(ml_dtypes.float4_e2m1fn).view(np.uint8) & 0xF
        words = (c[..., 0::2] | (c[..., 1::2] << 4)).reshape(k // 512, 128, 2 * n)
    return np.ascontiguousarray(words), np.ascontiguousarray(byte.astype(np.uint8).reshape(k // 512, 16, n))


def unpack_weight(words, scales, fmt):
    g, _, n = scales.shape
    words = np.ascontiguousarray(words).reshape(g, 128, n, -1)
    if fmt == "e4m3":
        vals = words.view(ml_dtypes.float8_e4m3fn).astype(np.float64)
    else:
        nib = np.empty((g, 128, n, 4), np.uint8)
        nib[..., 0::2] = words & 0xF
        nib[..., 1::2] = words >> 4
        vals = E2M1[nib]
    vals = vals * np.repeat(np.exp2(scales.astype(np.float64) - 127.0), 8, axis=1)[..., None]
    return vals.transpose(0, 1, 3, 2).reshape(g * 512, n)


def gelu(v):
    return 0.5 * v * (1.0 + np.tanh(np.sqrt(2.0 / np.pi) * (v + 0.044715 * v**3)))


def striped8(idx):
    return np.concatenate([v.reshape(-1, 16).T for v in idx]).astype(np.uint16)


def unstriped8(offs):
    return np.stack([offs[16 * g:16 * g + 16].T.reshape(-1) for g in range(8)]).astype(np.int64)


def heads(xT, wgt, idx8):
    k = np.arange(xT.shape[0])
    return wgt[k // 4 % 128] * xT[k[:, None], idx8[k % 512 // 64]]


K, T, S, H, N = 1024, 2048, 1024, 512, 768

def setup_inputs():
    n = np.random.standard_normal
    s = mx_kscale(K)[:, None]
    u = mx_kscale(H)[:, None]
    w2_words, w2_scales = pack_weight(n((H, N)) / np.sqrt(H) / u, "e2m1")
    gain = np.random.uniform(0.5, 1.5, H) * u[:, 0]
    return {
        "xT": (n((K, T)) * s).astype(np.float32),
        "wgt": np.repeat(np.random.uniform(0.5, 2.0, (8, S)), 16, axis=0).astype(np.float32),
        "offs": striped8(np.stack([np.random.permutation(T)[:S] for _ in range(8)])),
        "w1": (n((K, H)) / np.sqrt(K) / s).astype(np.float32),
        "gain": gain.astype(np.float32),
        "w2_words": w2_words,
        "w2_scales": w2_scales,
        "wm": (n((K, N)) / np.sqrt(K) / s).astype(np.float32),
        "bm": (0.5 * n(N)).astype(np.float32),
    }

def reference(xT, wgt, offs, w1, gain, w2_words, w2_scales, wm, bm):
    xg = mxq(heads(f64(xT), f64(wgt), unstriped8(offs)), 0, "e4m3")
    w1q = mxq(f64(w1), 0, "e4m3")
    wmq = mxq(f64(wm), 0, "e4m3")
    w2 = unpack_weight(w2_words, w2_scales, "e2m1")
    h = f64(gain)[:, None] * np.tanh(w1q.T @ xg)
    hq = mxq(h, 0, "e4m3")
    y = w2.T @ hq
    m = (wmq.T @ xg) + f64(bm)[:, None]
    return y * (1.0 / (1.0 + np.exp(-m)))

@@ -1,0 +1,243 @@
+from contextlib import ExitStack
+
+import concourse.mybir as mybir
+
+K, T, S, H, N = 1024, 2048, 1024, 512, 768
+FLOPS = 2 * S * (K * H + H * N + K * N)
+
+F32 = mybir.dt.float32
+BF16 = mybir.dt.bfloat16
+I32 = mybir.dt.int32
+U32 = mybir.dt.uint32
+U16 = mybir.dt.uint16
+U8 = mybir.dt.uint8
+FP8X4 = mybir.dt.float8_e4m3fn_x4
+FP4X4 = mybir.dt.float4_e2m1fn_x4
+MULT = mybir.AluOpType.mult
+ACT = mybir.ActivationFunctionType
+
+P = 128
+PACK = 4
+K_PASS = P * PACK
+PASSES = K // K_PASS
+CHUNK = 256
+H_CHUNK = 128
+BANK = 512
+
+
+def tile_list_masked_microphone_picks_kernel(tc, xT, wgt, offs, w1, gain, w2_words, w2_scales, wm, bm, out):
+    nc = tc.nc
+    with ExitStack() as ctx:
+        lists = ctx.enter_context(tc.tile_pool(name="lists", bufs=1))
+        keep = ctx.enter_context(tc.tile_pool(name="keep", bufs=1))
+        ring = ctx.enter_context(tc.tile_pool(name="ring", bufs=4))
+        psum = ctx.enter_context(tc.psum_pool(name="psum", bufs=1))
+
+        offsets = lists.tile([P, S // 16], U16, name="offsets")
+        planes = [[keep.tile([P, T], F32, name="plane%d%d" % (a, i), align_bytes=64) for i in range(PACK)] for a in range(PASSES)]
+        x_bf = [keep.tile([P, PACK * S], BF16, name="x_bf%d" % a, align_bytes=64) for a in range(PASSES)]
+        wm_bf = [keep.tile([P, PACK * N], BF16, name="wm_bf%d" % a, align_bytes=64) for a in range(PASSES)]
+        late = {}
+        weight = keep.tile([P, S], F32, name="weight")
+        picked = [keep.tile([P, PACK, S], F32, name="picked%d" % a) for a in range(PASSES)]
+        w1_raw = [keep.tile([P, PACK, H], F32, name="w1_raw%d" % a) for a in range(PASSES)]
+        wm_raw = [keep.tile([P, PACK, N], F32, name="wm_raw%d" % a) for a in range(PASSES)]
+        w1_bf = [keep.tile([P, PACK * H], BF16, name="w1_bf%d" % a, align_bytes=64) for a in range(PASSES)]
+        x_codes = keep.tile([P, PASSES, S], U32, name="x_codes", align_bytes=64)
+        x_scales = keep.tile([P, PASSES, S], U8, name="x_scales", align_bytes=64)
+        w1_codes = keep.tile([P, PASSES, H], U32, name="w1_codes", align_bytes=64)
+        w1_scales = keep.tile([P, PASSES, H], U8, name="w1_scales", align_bytes=64)
+        wm_codes = keep.tile([P, PASSES, N], U32, name="wm_codes", align_bytes=64)
+        wm_scales = keep.tile([P, PASSES, N], U8, name="wm_scales", align_bytes=64)
+        h_codes = keep.tile([P, S], U32, name="h_codes", align_bytes=64)
+        h_scales = keep.tile([P, S], U8, name="h_scales", align_bytes=64)
+        w2_codes = keep.tile([P, 2 * N], U8, name="w2_codes", align_bytes=64)
+        w2_plane = keep.tile([P, N], U8, name="w2_plane", align_bytes=64)
+        gain_sb = keep.tile([P, PACK], F32, name="gain_sb")
+        bm_sb = keep.tile([P, N // P], F32, name="bm_sb")
+        warm = keep.tile([P, 16], F32, name="warm")
+
+        def load_plane(a, i):
+            rows = xT[a * K_PASS : (a + 1) * K_PASS, :].rearrange("(p i) t -> p i t", i=PACK)
+            nc.sync.dma_start(out=planes[a][i][:], in_=rows[:, i, :])
+
+        def load_wgt(c0, c1):
+            nc.sync.dma_start(out=weight[:, c0:c1], in_=wgt[:, c0:c1])
+
+        def load_w1(a):
+            rows = w1[a * K_PASS : (a + 1) * K_PASS, :].rearrange("(p i) r -> p i r", i=PACK)
+            nc.sync.dma_start(out=w1_raw[a][:], in_=rows)
+
+        def load_wm(a, c0, c1):
+            rows = wm[a * K_PASS : (a + 1) * K_PASS, :].rearrange("(p i) n -> p i n", i=PACK)
+            nc.sync.dma_start(out=wm_raw[a][:, :, c0:c1], in_=rows[:, :, c0:c1])
+
+        def load_w2_scales(q):
+            nc.sync.dma_start(
+                out=w2_plane[32 * q : 32 * q + 4, :].bitcast(I32), in_=w2_scales[0, 4 * q : 4 * q + 4, :].bitcast(I32)
+            )
+
+        def load_w2_codes():
+            nc.sync.dma_start(out=w2_codes[:].bitcast(I32), in_=w2_words[0].bitcast(I32))
+
+        def load_gain():
+            nc.sync.dma_start(out=gain_sb[:], in_=gain.rearrange("(p t) -> p t", t=PACK))
+
+        def load_bm():
+            with nc.allow_non_contiguous_dma(reason="one bias value a partition"):
+                nc.sync.dma_start(out=bm_sb[:], in_=bm.rearrange("(c p) -> p c", p=P))
+
+        def copy_on(engine, dst, src):
+            if engine == "V":
+                nc.vector.tensor_copy(out=dst, in_=src)
+            else:
+                nc.scalar.copy(out=dst, in_=src)
+
+        def gather(a, i, j0, j1):
+            nc.vector.tensor_tensor(
+                picked[a][:, i, j0:j1], planes[a][i][:].indirect(offsets[:, j0 // 16 : j1 // 16]), weight[:, j0:j1], MULT
+            )
+
+        def interleave(engine, staged, raw, c0):
+            copy_on(
+                engine,
+                staged[:, PACK * c0 : PACK * (c0 + CHUNK)].rearrange("p (c i t) -> p c t i", i=4, t=PACK),
+                raw[:, :, c0 : c0 + CHUNK].rearrange("p t (c i) -> p c t i", i=4),
+            )
+
+        def interleave_pair(engine, staged, raw, c0, t0):
+            copy_on(
+                engine,
+                staged[:, PACK * c0 : PACK * (c0 + CHUNK)].rearrange("p (c i t) -> p c t i", i=4, t=PACK)[:, :, t0 : t0 + 2, :],
+                raw[:, t0 : t0 + 2, c0 : c0 + CHUNK].rearrange("p t (c i) -> p c t i", i=4),
+            )
+
+        def quantize(codes, scales, staged, c0, c1):
+            nc.vector.quantize_mx(out=codes[:, c0:c1].bitcast(FP8X4), scales=scales[:, c0:c1], in_=staged[:, PACK * c0 : PACK * c1])
+
+        def x_chunk(engine, a, c0):
+            interleave(engine, x_bf[a], picked[a], c0)
+            quantize(x_codes[:, a, :], x_scales[:, a, :], x_bf[a], c0, c0 + CHUNK)
+
+        def wm_chunk(engine, a, c0):
+            interleave(engine, wm_bf[a], wm_raw[a], c0)
+            quantize(wm_codes[:, a, :], wm_scales[:, a, :], wm_bf[a], c0, c0 + CHUNK)
+
+        def w1_cast(engine, a, m0, m1):
+            copy_on(
+                engine,
+                w1_bf[a][:].rearrange("p (t m i) -> p m i t", t=PACK, i=PACK)[:, m0:m1],
+                w1_raw[a][:].rearrange("p i (m t) -> p m i t", t=PACK)[:, m0:m1],
+            )
+
+        def w1_quant(a):
+            quantize(w1_codes[:, a, :], w1_scales[:, a, :], w1_bf[a], 0, H)
+
+        def mx(acc, wc, ws, xc, xs, start, stop, wdt=FP8X4):
+            nc.tensor.matmul_mx(
+                out=acc, lhsT=wc.bitcast(wdt), lhsT_scale=ws, rhs=xc.bitcast(FP8X4), rhs_scale=xs, start=start, stop=stop
+            )
+
+        def hidden(c0, width):
+            h_bf = late["h_bf"]
+            for j0 in range(c0, c0 + width, H_CHUNK):
+                js = slice(j0, j0 + H_CHUNK)
+                acc = psum.tile([P, PACK, H_CHUNK], F32, name="h_acc", tag="hy", bufs=4)
+                for t in range(PACK):
+                    ms = slice(t * P, (t + 1) * P)
+                    for a in range(PASSES):
+                        mx(acc[:, t, :], w1_codes[:, a, ms], w1_scales[:, a, ms], x_codes[:, a, js], x_scales[:, a, js],
+                           a == 0, a == PASSES - 1)
+                th = ring.tile([P, H_CHUNK, PACK], F32, name="th")
+                nc.scalar.activation(out=th[:], in_=acc[:].rearrange("p t j -> p j t"), func=ACT.Tanh)
+                nc.vector.tensor_tensor(
+                    h_bf[:, PACK * j0 : PACK * (j0 + H_CHUNK)].rearrange("p (j t) -> p j t", t=PACK),
+                    th[:],
+                    gain_sb[:].unsqueeze(1).to_broadcast([P, H_CHUNK, PACK]),
+                    MULT,
+                )
+            quantize(h_codes, h_scales, h_bf, c0, c0 + width)
+
+        def mask_of(n, j0, width=BANK):
+            ns = slice(n * P, (n + 1) * P)
+            js = slice(j0, j0 + width)
+            m_acc = psum.tile([P, BANK], F32, name="m_acc", bufs=4)
+            for a in range(PASSES):
+                mx(m_acc[:, 0:width], wm_codes[:, a, ns], wm_scales[:, a, ns], x_codes[:, a, js], x_scales[:, a, js],
+                   a == 0, a == PASSES - 1)
+            mask = late["mask"][n // 2][:, n % 2, js]
+            nc.scalar.activation(out=mask, in_=m_acc[:, 0:width], func=ACT.Sigmoid, bias=bm_sb[:, n : n + 1])
+
+        def finish(n, j0, width=BANK):
+            ns = slice(n * P, (n + 1) * P)
+            js = slice(j0, j0 + width)
+            y_acc = psum.tile([P, BANK], F32, name="y_acc", tag="hy", bufs=4)
+            mx(y_acc[:, 0:width], w2_codes[:, 2 * n * P : 2 * (n + 1) * P], w2_plane[:, ns], h_codes[:, js], h_scales[:, js],
+               True, True, FP4X4)
+            mask = late["mask"][n // 2][:, n % 2, js]
+            nc.vector.tensor_tensor(mask, y_acc[:, 0:width], mask, MULT)
+            nc.sync.dma_start(out=out[ns, js], in_=mask)
+
+        def late_tiles():
+            late["mask"] = [keep.tile([P, 2, S], F32, name="mask%d" % i, tag="plane0%d" % i, align_bytes=64) for i in range(3)]
+            late["h_bf"] = keep.tile([P, PACK * S], BF16, name="h_bf", tag="plane03", align_bytes=64)
+
+        nc.sync.dma_start(offsets[:], offs)
+        nc.gpsimd.memset(w2_plane[:].bitcast(I32), 0)
+        nc.gpsimd.memset(warm[:, 0:8], 0.0)
+        nc.scalar.activation(out=warm[:, 8:16], in_=warm[:, 0:8], func=ACT.Sigmoid)
+        load_wgt(0, 512)
+        load_plane(0, 0)
+        load_wgt(512, 1024)
+        for i in range(1, PACK):
+            load_plane(0, i)
+        for i in range(PACK - 1):
+            load_plane(1, i)
+        load_w1(0)
+        load_plane(1, 3)
+        load_w1(1)
+        load_gain()
+        load_wm(0, 0, 256)
+        load_wm(1, 0, 256)
+        load_bm()
+        load_wm(0, 256, 512)
+        load_wm(1, 256, 512)
+        load_w2_codes()
+        load_wm(0, 512, 768)
+        load_wm(1, 512, 768)
+        for q in range(4):
+            load_w2_scales(q)
+
+        def gathers(a, i, width):
+            for j0 in range(0, S, width):
+                gather(a, i, j0, j0 + width)
+
+        for i in range(PACK - 1):
+            gathers(0, i, 512)
+        gathers(0, PACK - 1, CHUNK)
+        late_tiles()
+        for i in range(PACK - 1):
+            gathers(1, i, 512)
+        for c0 in range(0, S, CHUNK):
+            x_chunk("S", 0, c0)
+        gathers(1, PACK - 1, CHUNK)
+        w1_cast("S", 0, 0, 64)
+        w1_cast("S", 0, 64, 128)
+        w1_quant(0)
+        w1_cast("V", 1, 0, 64)
+        w1_cast("V", 1, 64, 128)
+        w1_quant(1)
+        for c0 in range(0, S, CHUNK):
+            x_chunk("S", 1, c0)
+        wm_chunk("V", 0, 0)
+        wm_chunk("S", 1, 0)
+        hidden(0, 512)
+        wm_chunk("V", 0, 256)
+        wm_chunk("S", 1, 256)
+        hidden(512, 512)
+        wm_chunk("V", 0, 512)
+        wm_chunk("S", 1, 512)
+        for j0 in range(0, S, BANK):
+            for n in range(N // P):
+                mask_of(n, j0)
+                finish(n, j0)

@@ -25,52 +25,60 @@ H_CHUNK = 128
 BANK = 512
 
 
+HOST = {"mask0":"plane00","mask1":"plane01","mask2":"plane02","h_bf0":"plane03","w1_codes0":"plane12","x_codes1_512":"w1_bf1","th0":"wm_raw1_0"}
+X_QUANT = [512,512]
+
+
 def tile_list_masked_microphone_picks_kernel(tc, xT, wgt, offs, w1, gain, w2_words, w2_scales, wm, bm, out):
     nc = tc.nc
     with ExitStack() as ctx:
         lists = ctx.enter_context(tc.tile_pool(name="lists", bufs=1))
         keep = ctx.enter_context(tc.tile_pool(name="keep", bufs=1))
-        ring = ctx.enter_context(tc.tile_pool(name="ring", bufs=4))
-        psum = ctx.enter_context(tc.psum_pool(name="psum", bufs=1))
-
+        psum = ctx.enter_context(tc.psum_pool(name="psum", bufs=8))
         offsets = lists.tile([P, S // 16], U16, name="offsets")
-        planes = [[keep.tile([P, T], F32, name="plane%d%d" % (a, i), align_bytes=64) for i in range(PACK)] for a in range(PASSES)]
-        x_bf = [keep.tile([P, PACK * S], BF16, name="x_bf%d" % a, align_bytes=64) for a in range(PASSES)]
-        wm_bf = [keep.tile([P, PACK * N], BF16, name="wm_bf%d" % a, align_bytes=64) for a in range(PASSES)]
-        late = {}
-        weight = keep.tile([P, S], F32, name="weight")
-        picked = [keep.tile([P, PACK, S], F32, name="picked%d" % a) for a in range(PASSES)]
-        w1_raw = [keep.tile([P, PACK, H], F32, name="w1_raw%d" % a) for a in range(PASSES)]
-        wm_raw = [keep.tile([P, PACK, N], F32, name="wm_raw%d" % a) for a in range(PASSES)]
-        w1_bf = [keep.tile([P, PACK * H], BF16, name="w1_bf%d" % a, align_bytes=64) for a in range(PASSES)]
-        x_codes = keep.tile([P, PASSES, S], U32, name="x_codes", align_bytes=64)
-        x_scales = keep.tile([P, PASSES, S], U8, name="x_scales", align_bytes=64)
-        w1_codes = keep.tile([P, PASSES, H], U32, name="w1_codes", align_bytes=64)
-        w1_scales = keep.tile([P, PASSES, H], U8, name="w1_scales", align_bytes=64)
-        wm_codes = keep.tile([P, PASSES, N], U32, name="wm_codes", align_bytes=64)
-        wm_scales = keep.tile([P, PASSES, N], U8, name="wm_scales", align_bytes=64)
-        h_codes = keep.tile([P, S], U32, name="h_codes", align_bytes=64)
-        h_scales = keep.tile([P, S], U8, name="h_scales", align_bytes=64)
-        w2_codes = keep.tile([P, 2 * N], U8, name="w2_codes", align_bytes=64)
-        w2_plane = keep.tile([P, N], U8, name="w2_plane", align_bytes=64)
-        gain_sb = keep.tile([P, PACK], F32, name="gain_sb")
-        bm_sb = keep.tile([P, N // P], F32, name="bm_sb")
-        warm = keep.tile([P, 16], F32, name="warm")
+        made = {}
+
+        def tile(name, shape, dtype):
+            if name not in made:
+                made[name] = keep.tile(shape, dtype, name=name, tag=HOST.get(name, name), align_bytes=64)
+            return made[name]
+
+        weight = tile("weight", [P, S], F32)
+        x_scales = tile("x_scales", [P, PASSES, S], U8)
+        w1_scales = tile("w1_scales", [P, PASSES, H], U8)
+        wm_scales = tile("wm_scales", [P, PASSES, N], U8)
+        h_codes = tile("h_codes", [P, S], U32)
+        h_scales = tile("h_scales", [P, S], U8)
+        w2_codes = tile("w2_codes", [P, 2 * N], U8)
+        w2_plane = tile("w2_plane", [P, N], U8)
+        gain_sb = tile("gain_sb", [P, PACK], F32)
+        bm_sb = tile("bm_sb", [P, N // P], F32)
+        warm = tile("warm", [P, 16], F32)
+        wm_raw = {}
+
+        def plane(a, i):
+            return tile("plane%d%d" % (a, i), [P, T], F32)
+
+        def picked(a):
+            return tile("picked%d" % a, [P, PACK, S], F32)
 
         def load_plane(a, i):
             rows = xT[a * K_PASS : (a + 1) * K_PASS, :].rearrange("(p i) t -> p i t", i=PACK)
-            nc.sync.dma_start(out=planes[a][i][:], in_=rows[:, i, :])
+            nc.sync.dma_start(out=plane(a, i)[:], in_=rows[:, i, :])
 
         def load_wgt(c0, c1):
             nc.sync.dma_start(out=weight[:, c0:c1], in_=wgt[:, c0:c1])
 
         def load_w1(a):
             rows = w1[a * K_PASS : (a + 1) * K_PASS, :].rearrange("(p i) r -> p i r", i=PACK)
-            nc.sync.dma_start(out=w1_raw[a][:], in_=rows)
+            nc.sync.dma_start(out=tile("w1_raw%d" % a, [P, PACK, H], F32)[:], in_=rows)
 
         def load_wm(a, c0, c1):
             rows = wm[a * K_PASS : (a + 1) * K_PASS, :].rearrange("(p i) n -> p i n", i=PACK)
-            nc.sync.dma_start(out=wm_raw[a][:, :, c0:c1], in_=rows[:, :, c0:c1])
+            piece = tile("wm_raw%d_%d" % (a, c0), [P, PACK, c1 - c0], F32)
+            nc.sync.dma_start(out=piece[:], in_=rows[:, :, c0:c1])
+            for c in range(c0, c1, CHUNK):
+                wm_raw[(a, c)] = piece[:, :, c - c0 : c - c0 + CHUNK]
 
         def load_w2_scales(q):
             nc.sync.dma_start(
@@ -95,149 +103,210 @@ def tile_list_masked_microphone_picks_kernel(tc, xT, wgt, offs, w1, gain, w2_wor
 
         def gather(a, i, j0, j1):
             nc.vector.tensor_tensor(
-                picked[a][:, i, j0:j1], planes[a][i][:].indirect(offsets[:, j0 // 16 : j1 // 16]), weight[:, j0:j1], MULT
+                picked(a)[:, i, j0:j1], plane(a, i)[:].indirect(offsets[:, j0 // 16 : j1 // 16]), weight[:, j0:j1], MULT
             )
 
-        def interleave(engine, staged, raw, c0):
+        def quantize(codes, scales, staged):
+            nc.vector.quantize_mx(out=codes.bitcast(FP8X4), scales=scales, in_=staged)
+
+        def x_bf(a, c0):
+            g0 = c0 // X_QUANT[a] * X_QUANT[a]
+            return tile("x_bf%d_%d" % (a, g0), [P, PACK * X_QUANT[a]], BF16), c0 - g0
+
+        def x_codes(a, j0):
+            return tile("x_codes%d_%d" % (a, j0 // BANK * BANK), [P, BANK], U32)
+
+        def wm_codes(a, c0):
+            return tile("wm_codes%d_%d" % (a, c0 // CHUNK * CHUNK), [P, CHUNK], U32)
+
+        def x_cast(engine, a, c0, t0, t1):
+            staged, at = x_bf(a, c0)
+            dst = staged[:, PACK * at : PACK * (at + CHUNK)].rearrange("p (c i t) -> p c t i", i=4, t=PACK)
+            src = picked(a)[:, t0:t1, c0 : c0 + CHUNK].rearrange("p t (c i) -> p c t i", i=4)
+            copy_on(engine, dst[:, :, t0:t1], src)
+
+        def x_quant(a, c0):
+            width = X_QUANT[a]
+            quantize(x_codes(a, c0)[:, c0 % BANK : c0 % BANK + width], x_scales[:, a, c0 : c0 + width], x_bf(a, c0)[0][:])
+
+        def wm_cast(engine, a, c0):
+            staged = tile("wm_bf%d_%d" % (a, c0), [P, PACK * CHUNK], BF16)
+            copy_on(engine, staged[:].rearrange("p (c i t) -> p c t i", i=4, t=PACK), wm_raw[(a, c0)].rearrange("p t (c i) -> p c t i", i=4))
+
+        def wm_quant(a, c0):
+            quantize(wm_codes(a, c0)[:], wm_scales[:, a, c0 : c0 + CHUNK], made["wm_bf%d_%d" % (a, c0)][:])
+
+        def w1_cast(engine, a, t0):
             copy_on(
                 engine,
-                staged[:, PACK * c0 : PACK * (c0 + CHUNK)].rearrange("p (c i t) -> p c t i", i=4, t=PACK),
-                raw[:, :, c0 : c0 + CHUNK].rearrange("p t (c i) -> p c t i", i=4),
-            )
-
-        def interleave_pair(engine, staged, raw, c0, t0):
-            copy_on(
-                engine,
-                staged[:, PACK * c0 : PACK * (c0 + CHUNK)].rearrange("p (c i t) -> p c t i", i=4, t=PACK)[:, :, t0 : t0 + 2, :],
-                raw[:, t0 : t0 + 2, c0 : c0 + CHUNK].rearrange("p t (c i) -> p c t i", i=4),
-            )
-
-        def quantize(codes, scales, staged, c0, c1):
-            nc.vector.quantize_mx(out=codes[:, c0:c1].bitcast(FP8X4), scales=scales[:, c0:c1], in_=staged[:, PACK * c0 : PACK * c1])
-
-        def x_chunk(engine, a, c0):
-            interleave(engine, x_bf[a], picked[a], c0)
-            quantize(x_codes[:, a, :], x_scales[:, a, :], x_bf[a], c0, c0 + CHUNK)
-
-        def wm_chunk(engine, a, c0):
-            interleave(engine, wm_bf[a], wm_raw[a], c0)
-            quantize(wm_codes[:, a, :], wm_scales[:, a, :], wm_bf[a], c0, c0 + CHUNK)
-
-        def w1_cast(engine, a, m0, m1):
-            copy_on(
-                engine,
-                w1_bf[a][:].rearrange("p (t m i) -> p m i t", t=PACK, i=PACK)[:, m0:m1],
-                w1_raw[a][:].rearrange("p i (m t) -> p m i t", t=PACK)[:, m0:m1],
+                tile("w1_bf%d" % a, [P, PACK * H], BF16)[:].rearrange("p (t m i) -> p m i t", t=PACK, i=PACK)[:, :, :, t0 : t0 + 2],
+                made["w1_raw%d" % a][:].rearrange("p i (m t) -> p m i t", t=PACK)[:, :, :, t0 : t0 + 2],
             )
 
         def w1_quant(a):
-            quantize(w1_codes[:, a, :], w1_scales[:, a, :], w1_bf[a], 0, H)
+            quantize(tile("w1_codes%d" % a, [P, H], U32)[:], w1_scales[:, a, :], made["w1_bf%d" % a][:])
 
         def mx(acc, wc, ws, xc, xs, start, stop, wdt=FP8X4):
             nc.tensor.matmul_mx(
                 out=acc, lhsT=wc.bitcast(wdt), lhsT_scale=ws, rhs=xc.bitcast(FP8X4), rhs_scale=xs, start=start, stop=stop
             )
 
-        def hidden(c0, width):
-            h_bf = late["h_bf"]
-            for j0 in range(c0, c0 + width, H_CHUNK):
-                js = slice(j0, j0 + H_CHUNK)
-                acc = psum.tile([P, PACK, H_CHUNK], F32, name="h_acc", tag="hy", bufs=4)
-                for t in range(PACK):
-                    ms = slice(t * P, (t + 1) * P)
-                    for a in range(PASSES):
-                        mx(acc[:, t, :], w1_codes[:, a, ms], w1_scales[:, a, ms], x_codes[:, a, js], x_scales[:, a, js],
-                           a == 0, a == PASSES - 1)
-                th = ring.tile([P, H_CHUNK, PACK], F32, name="th")
-                nc.scalar.activation(out=th[:], in_=acc[:].rearrange("p t j -> p j t"), func=ACT.Tanh)
-                nc.vector.tensor_tensor(
-                    h_bf[:, PACK * j0 : PACK * (j0 + H_CHUNK)].rearrange("p (j t) -> p j t", t=PACK),
-                    th[:],
-                    gain_sb[:].unsqueeze(1).to_broadcast([P, H_CHUNK, PACK]),
-                    MULT,
-                )
-            quantize(h_codes, h_scales, h_bf, c0, c0 + width)
-
-        def mask_of(n, j0, width=BANK):
-            ns = slice(n * P, (n + 1) * P)
-            js = slice(j0, j0 + width)
-            m_acc = psum.tile([P, BANK], F32, name="m_acc", bufs=4)
+        def hidden(t, j0):
+            js = slice(j0, j0 + BANK)
+            ms = slice(t * P, (t + 1) * P)
+            acc = psum.tile([P, BANK], F32, name="acc")
             for a in range(PASSES):
-                mx(m_acc[:, 0:width], wm_codes[:, a, ns], wm_scales[:, a, ns], x_codes[:, a, js], x_scales[:, a, js],
+                mx(acc[:], made["w1_codes%d" % a][:, ms], w1_scales[:, a, ms], x_codes(a, j0)[:], x_scales[:, a, js],
                    a == 0, a == PASSES - 1)
-            mask = late["mask"][n // 2][:, n % 2, js]
-            nc.scalar.activation(out=mask, in_=m_acc[:, 0:width], func=ACT.Sigmoid, bias=bm_sb[:, n : n + 1])
+            nc.scalar.activation(out=tile("th%d" % j0, [P, PACK, BANK], F32)[:, t, :], in_=acc[:], func=ACT.Tanh)
 
-        def finish(n, j0, width=BANK):
+        def gained(j0, width):
+            c0 = j0 % BANK
+            h_bf = tile("h_bf%d" % (j0 - c0), [P, PACK * BANK], BF16)
+            nc.vector.tensor_tensor(
+                h_bf[:, PACK * c0 : PACK * (c0 + width)].rearrange("p (c i t) -> p c t i", i=4, t=PACK),
+                made["th%d" % (j0 - c0)][:, :, c0 : c0 + width].rearrange("p t (c i) -> p c t i", i=4),
+                gain_sb[:].unsqueeze(1).unsqueeze(3).to_broadcast([P, width // 4, PACK, 4]),
+                MULT,
+            )
+
+        def h_quant(j0, width):
+            c0 = j0 % BANK
+            quantize(h_codes[:, j0 : j0 + width], h_scales[:, j0 : j0 + width],
+                     made["h_bf%d" % (j0 - c0)][:, PACK * c0 : PACK * (c0 + width)])
+
+        def mask_of(n, j0, width):
             ns = slice(n * P, (n + 1) * P)
             js = slice(j0, j0 + width)
-            y_acc = psum.tile([P, BANK], F32, name="y_acc", tag="hy", bufs=4)
-            mx(y_acc[:, 0:width], w2_codes[:, 2 * n * P : 2 * (n + 1) * P], w2_plane[:, ns], h_codes[:, js], h_scales[:, js],
+            acc = psum.tile([P, BANK], F32, name="acc")
+            for a in range(PASSES):
+                mx(acc[:, 0:width], wm_codes(a, n * P)[:, n % 2 * P : (n % 2 + 1) * P], wm_scales[:, a, ns],
+                   x_codes(a, j0)[:, j0 % BANK : j0 % BANK + width], x_scales[:, a, js], a == 0, a == PASSES - 1)
+            mask = tile("mask%d" % (n // 2), [P, 2, S], F32)[:, n % 2, js]
+            nc.scalar.activation(out=mask, in_=acc[:, 0:width], func=ACT.Sigmoid, bias=bm_sb[:, n : n + 1])
+
+        def finish(n, j0, width):
+            ns = slice(n * P, (n + 1) * P)
+            js = slice(j0, j0 + width)
+            acc = psum.tile([P, BANK], F32, name="acc")
+            mx(acc[:, 0:width], w2_codes[:, 2 * n * P : 2 * (n + 1) * P], w2_plane[:, ns], h_codes[:, js], h_scales[:, js],
                True, True, FP4X4)
-            mask = late["mask"][n // 2][:, n % 2, js]
-            nc.vector.tensor_tensor(mask, y_acc[:, 0:width], mask, MULT)
+            mask = made["mask%d" % (n // 2)][:, n % 2, js]
+            nc.vector.tensor_tensor(mask, acc[:, 0:width], mask, MULT)
             nc.sync.dma_start(out=out[ns, js], in_=mask)
 
-        def late_tiles():
-            late["mask"] = [keep.tile([P, 2, S], F32, name="mask%d" % i, tag="plane0%d" % i, align_bytes=64) for i in range(3)]
-            late["h_bf"] = keep.tile([P, PACK * S], BF16, name="h_bf", tag="plane03", align_bytes=64)
-
-        nc.sync.dma_start(offsets[:], offs)
         nc.gpsimd.memset(w2_plane[:].bitcast(I32), 0)
         nc.gpsimd.memset(warm[:, 0:8], 0.0)
         nc.scalar.activation(out=warm[:, 8:16], in_=warm[:, 0:8], func=ACT.Sigmoid)
-        load_wgt(0, 512)
         load_plane(0, 0)
+        nc.sync.dma_start(offsets[:], offs)
+        load_wgt(0, 512)
         load_wgt(512, 1024)
-        for i in range(1, PACK):
-            load_plane(0, i)
-        for i in range(PACK - 1):
-            load_plane(1, i)
+        load_plane(0, 1)
+        load_plane(0, 2)
+        load_plane(0, 3)
+        load_plane(1, 0)
+        load_plane(1, 1)
         load_w1(0)
+        load_plane(1, 2)
         load_plane(1, 3)
         load_w1(1)
-        load_gain()
-        load_wm(0, 0, 256)
-        load_wm(1, 0, 256)
+        load_wm(1, 0, 512)
+        load_wm(0, 0, 512)
         load_bm()
-        load_wm(0, 256, 512)
-        load_wm(1, 256, 512)
-        load_w2_codes()
         load_wm(0, 512, 768)
+        load_gain()
         load_wm(1, 512, 768)
-        for q in range(4):
-            load_w2_scales(q)
-
-        def gathers(a, i, width):
-            for j0 in range(0, S, width):
-                gather(a, i, j0, j0 + width)
-
-        for i in range(PACK - 1):
-            gathers(0, i, 512)
-        gathers(0, PACK - 1, CHUNK)
-        late_tiles()
-        for i in range(PACK - 1):
-            gathers(1, i, 512)
-        for c0 in range(0, S, CHUNK):
-            x_chunk("S", 0, c0)
-        gathers(1, PACK - 1, CHUNK)
-        w1_cast("S", 0, 0, 64)
-        w1_cast("S", 0, 64, 128)
+        load_w2_scales(0)
+        load_w2_scales(1)
+        load_w2_scales(2)
+        load_w2_scales(3)
+        load_w2_codes()
+        gather(0, 0, 0, 512)
+        gather(0, 0, 512, 1024)
+        gather(0, 1, 0, 512)
+        gather(0, 1, 512, 1024)
+        gather(0, 2, 0, 512)
+        gather(0, 2, 512, 1024)
+        gather(0, 3, 0, 512)
+        gather(0, 3, 512, 1024)
+        gather(1, 0, 0, 512)
+        gather(1, 0, 512, 1024)
+        gather(1, 1, 0, 512)
+        gather(1, 1, 512, 1024)
+        gather(1, 2, 0, 512)
+        gather(1, 2, 512, 1024)
+        gather(1, 3, 0, 256)
+        gather(1, 3, 256, 512)
+        gather(1, 3, 512, 768)
+        gather(1, 3, 768, 1024)
+        x_cast("S", 0, 0, 0, 4)
+        x_cast("S", 0, 256, 0, 4)
+        x_quant(0, 0)
+        x_cast("S", 0, 512, 0, 4)
+        x_cast("S", 0, 768, 0, 4)
+        x_quant(0, 512)
+        w1_cast("S", 0, 0)
+        w1_cast("S", 0, 2)
         w1_quant(0)
-        w1_cast("V", 1, 0, 64)
-        w1_cast("V", 1, 64, 128)
+        x_cast("S", 1, 0, 0, 4)
+        x_cast("V", 1, 256, 0, 4)
+        x_quant(1, 0)
+        w1_cast("S", 1, 0)
+        w1_cast("S", 1, 2)
         w1_quant(1)
-        for c0 in range(0, S, CHUNK):
-            x_chunk("S", 1, c0)
-        wm_chunk("V", 0, 0)
-        wm_chunk("S", 1, 0)
+        x_cast("V", 1, 512, 0, 4)
+        x_cast("V", 1, 768, 0, 4)
+        x_quant(1, 512)
+        wm_cast("V", 0, 0)
+        wm_quant(0, 0)
+        wm_cast("S", 1, 0)
+        wm_quant(1, 0)
+        wm_cast("V", 0, 256)
+        wm_quant(0, 256)
+        wm_cast("V", 1, 256)
+        wm_quant(1, 256)
+        hidden(0, 0)
+        hidden(1, 0)
+        hidden(2, 0)
+        hidden(3, 0)
+        gained(0, 256)
+        h_quant(0, 256)
+        gained(256, 256)
+        h_quant(256, 256)
         hidden(0, 512)
-        wm_chunk("V", 0, 256)
-        wm_chunk("S", 1, 256)
-        hidden(512, 512)
-        wm_chunk("V", 0, 512)
-        wm_chunk("S", 1, 512)
-        for j0 in range(0, S, BANK):
-            for n in range(N // P):
-                mask_of(n, j0)
-                finish(n, j0)
+        hidden(1, 512)
+        hidden(2, 512)
+        hidden(3, 512)
+        gained(512, 256)
+        h_quant(512, 256)
+        gained(768, 256)
+        h_quant(768, 256)
+        mask_of(0, 0, 512)
+        mask_of(1, 0, 512)
+        finish(0, 0, 512)
+        mask_of(2, 0, 512)
+        finish(1, 0, 512)
+        mask_of(3, 0, 512)
+        finish(2, 0, 512)
+        mask_of(0, 512, 512)
+        finish(3, 0, 512)
+        wm_cast("S", 0, 512)
+        wm_quant(0, 512)
+        wm_cast("S", 1, 512)
+        wm_quant(1, 512)
+        mask_of(1, 512, 512)
+        finish(0, 512, 512)
+        mask_of(2, 512, 512)
+        finish(1, 512, 512)
+        mask_of(3, 512, 512)
+        finish(2, 512, 512)
+        mask_of(4, 0, 512)
+        finish(3, 512, 512)
+        mask_of(5, 0, 512)
+        finish(4, 0, 512)
+        mask_of(4, 512, 512)
+        finish(5, 0, 512)
+        mask_of(5, 512, 512)
+        finish(4, 512, 512)
+        finish(5, 512, 512)

@@ -25,7 +25,7 @@ H_CHUNK = 128
 BANK = 512
 
 
-HOST = {"mask0":"plane00","mask1":"plane01","mask2":"plane02","h_bf0":"plane03","w1_codes0":"plane12","x_codes1_512":"w1_bf1","th0":"wm_raw1_0"}
+HOST = {"mask0":"plane00","mask1":"plane01","mask2":"plane02","h_bf0":"plane03","w1_codes0":"plane13","x_codes0_512":"plane12","x_codes1_512":"w1_bf1","th0":"wm_raw1_0"}
 X_QUANT = [512,512]
 
 
@@ -151,22 +151,24 @@ def tile_list_masked_microphone_picks_kernel(tc, xT, wgt, offs, w1, gain, w2_wor
                 out=acc, lhsT=wc.bitcast(wdt), lhsT_scale=ws, rhs=xc.bitcast(FP8X4), rhs_scale=xs, start=start, stop=stop
             )
 
-        def hidden(t, j0):
-            js = slice(j0, j0 + BANK)
-            ms = slice(t * P, (t + 1) * P)
-            acc = psum.tile([P, BANK], F32, name="acc")
-            for a in range(PASSES):
-                mx(acc[:], made["w1_codes%d" % a][:, ms], w1_scales[:, a, ms], x_codes(a, j0)[:], x_scales[:, a, js],
-                   a == 0, a == PASSES - 1)
-            nc.scalar.activation(out=tile("th%d" % j0, [P, PACK, BANK], F32)[:, t, :], in_=acc[:], func=ACT.Tanh)
+        def hidden(j0):
+            c0 = j0 % BANK
+            acc = psum.tile([P, PACK, H_CHUNK], F32, name="acc")
+            for t in range(PACK):
+                ms = slice(t * P, (t + 1) * P)
+                for a in range(PASSES):
+                    mx(acc[:, t, :], made["w1_codes%d" % a][:, ms], w1_scales[:, a, ms], x_codes(a, j0)[:, c0 : c0 + H_CHUNK],
+                       x_scales[:, a, j0 : j0 + H_CHUNK], a == 0, a == PASSES - 1)
+            th = tile("th%d" % (j0 - c0), [P, BANK, PACK], F32)
+            nc.scalar.activation(out=th[:, c0 : c0 + H_CHUNK, :], in_=acc[:].rearrange("p t j -> p j t"), func=ACT.Tanh)
 
         def gained(j0, width):
             c0 = j0 % BANK
             h_bf = tile("h_bf%d" % (j0 - c0), [P, PACK * BANK], BF16)
             nc.vector.tensor_tensor(
-                h_bf[:, PACK * c0 : PACK * (c0 + width)].rearrange("p (c i t) -> p c t i", i=4, t=PACK),
-                made["th%d" % (j0 - c0)][:, :, c0 : c0 + width].rearrange("p t (c i) -> p c t i", i=4),
-                gain_sb[:].unsqueeze(1).unsqueeze(3).to_broadcast([P, width // 4, PACK, 4]),
+                h_bf[:, PACK * c0 : PACK * (c0 + width)].rearrange("p (j t) -> p j t", t=PACK),
+                made["th%d" % (j0 - c0)][:, c0 : c0 + width, :],
+                gain_sb[:].unsqueeze(1).to_broadcast([P, width, PACK]),
                 MULT,
             )
 
@@ -207,8 +209,8 @@ def tile_list_masked_microphone_picks_kernel(tc, xT, wgt, offs, w1, gain, w2_wor
         load_plane(0, 3)
         load_plane(1, 0)
         load_plane(1, 1)
-        load_w1(0)
         load_plane(1, 2)
+        load_w1(0)
         load_plane(1, 3)
         load_w1(1)
         load_wm(1, 0, 512)
@@ -264,23 +266,27 @@ def tile_list_masked_microphone_picks_kernel(tc, xT, wgt, offs, w1, gain, w2_wor
         wm_quant(1, 0)
         wm_cast("V", 0, 256)
         wm_quant(0, 256)
-        wm_cast("V", 1, 256)
+        wm_cast("S", 1, 256)
         wm_quant(1, 256)
-        hidden(0, 0)
-        hidden(1, 0)
-        hidden(2, 0)
-        hidden(3, 0)
-        gained(0, 256)
+        hidden(0)
+        gained(0, 128)
+        hidden(128)
+        gained(128, 128)
         h_quant(0, 256)
-        gained(256, 256)
+        hidden(256)
+        gained(256, 128)
+        hidden(384)
+        gained(384, 128)
         h_quant(256, 256)
-        hidden(0, 512)
-        hidden(1, 512)
-        hidden(2, 512)
-        hidden(3, 512)
-        gained(512, 256)
+        hidden(512)
+        gained(512, 128)
+        hidden(640)
+        gained(640, 128)
         h_quant(512, 256)
-        gained(768, 256)
+        hidden(768)
+        gained(768, 128)
+        hidden(896)
+        gained(896, 128)
         h_quant(768, 256)
         mask_of(0, 0, 512)
         mask_of(1, 0, 512)

from contextlib import ExitStack

import concourse.mybir as mybir

K, T, S, H, N = 1024, 2048, 1024, 512, 768
FLOPS = 2 * S * (K * H + H * N + K * N)

F32 = mybir.dt.float32
BF16 = mybir.dt.bfloat16
I32 = mybir.dt.int32
U32 = mybir.dt.uint32
U16 = mybir.dt.uint16
U8 = mybir.dt.uint8
FP8X4 = mybir.dt.float8_e4m3fn_x4
FP4X4 = mybir.dt.float4_e2m1fn_x4
MULT = mybir.AluOpType.mult
ACT = mybir.ActivationFunctionType

P = 128
PACK = 4
K_PASS = P * PACK
PASSES = K // K_PASS
CHUNK = 256
H_CHUNK = 128
BANK = 512


HOST = {"mask0":"plane00","mask1":"plane01","mask2":"plane02","h_bf0":"plane03","w1_codes0":"plane13","x_codes0_512":"plane12","x_codes1_512":"w1_bf1","th0":"wm_raw1_0"}
X_QUANT = [512,512]


def tile_list_masked_microphone_picks_kernel(tc, xT, wgt, offs, w1, gain, w2_words, w2_scales, wm, bm, out):
    nc = tc.nc
    with ExitStack() as ctx:
        lists = ctx.enter_context(tc.tile_pool(name="lists", bufs=1))
        keep = ctx.enter_context(tc.tile_pool(name="keep", bufs=1))
        psum = ctx.enter_context(tc.psum_pool(name="psum", bufs=8))
        offsets = lists.tile([P, S // 16], U16, name="offsets")
        made = {}

        def tile(name, shape, dtype):
            if name not in made:
                made[name] = keep.tile(shape, dtype, name=name, tag=HOST.get(name, name), align_bytes=64)
            return made[name]

        weight = tile("weight", [P, S], F32)
        x_scales = tile("x_scales", [P, PASSES, S], U8)
        w1_scales = tile("w1_scales", [P, PASSES, H], U8)
        wm_scales = tile("wm_scales", [P, PASSES, N], U8)
        h_codes = tile("h_codes", [P, S], U32)
        h_scales = tile("h_scales", [P, S], U8)
        w2_codes = tile("w2_codes", [P, 2 * N], U8)
        w2_plane = tile("w2_plane", [P, N], U8)
        gain_sb = tile("gain_sb", [P, PACK], F32)
        bm_sb = tile("bm_sb", [P, N // P], F32)
        warm = tile("warm", [P, 16], F32)
        wm_raw = {}

        def plane(a, i):
            return tile("plane%d%d" % (a, i), [P, T], F32)

        def picked(a):
            return tile("picked%d" % a, [P, PACK, S], F32)

        def load_plane(a, i):
            rows = xT[a * K_PASS : (a + 1) * K_PASS, :].rearrange("(p i) t -> p i t", i=PACK)
            nc.sync.dma_start(out=plane(a, i)[:], in_=rows[:, i, :])

        def load_wgt(c0, c1):
            nc.sync.dma_start(out=weight[:, c0:c1], in_=wgt[:, c0:c1])

        def load_w1(a):
            rows = w1[a * K_PASS : (a + 1) * K_PASS, :].rearrange("(p i) r -> p i r", i=PACK)
            nc.sync.dma_start(out=tile("w1_raw%d" % a, [P, PACK, H], F32)[:], in_=rows)

        def load_wm(a, c0, c1):
            rows = wm[a * K_PASS : (a + 1) * K_PASS, :].rearrange("(p i) n -> p i n", i=PACK)
            piece = tile("wm_raw%d_%d" % (a, c0), [P, PACK, c1 - c0], F32)
            nc.sync.dma_start(out=piece[:], in_=rows[:, :, c0:c1])
            for c in range(c0, c1, CHUNK):
                wm_raw[(a, c)] = piece[:, :, c - c0 : c - c0 + CHUNK]

        def load_w2_scales(q):
            nc.sync.dma_start(
                out=w2_plane[32 * q : 32 * q + 4, :].bitcast(I32), in_=w2_scales[0, 4 * q : 4 * q + 4, :].bitcast(I32)
            )

        def load_w2_codes():
            nc.sync.dma_start(out=w2_codes[:].bitcast(I32), in_=w2_words[0].bitcast(I32))

        def load_gain():
            nc.sync.dma_start(out=gain_sb[:], in_=gain.rearrange("(p t) -> p t", t=PACK))

        def load_bm():
            with nc.allow_non_contiguous_dma(reason="one bias value a partition"):
                nc.sync.dma_start(out=bm_sb[:], in_=bm.rearrange("(c p) -> p c", p=P))

        def copy_on(engine, dst, src):
            if engine == "V":
                nc.vector.tensor_copy(out=dst, in_=src)
            else:
                nc.scalar.copy(out=dst, in_=src)

        def gather(a, i, j0, j1):
            nc.vector.tensor_tensor(
                picked(a)[:, i, j0:j1], plane(a, i)[:].indirect(offsets[:, j0 // 16 : j1 // 16]), weight[:, j0:j1], MULT
            )

        def quantize(codes, scales, staged):
            nc.vector.quantize_mx(out=codes.bitcast(FP8X4), scales=scales, in_=staged)

        def x_bf(a, c0):
            g0 = c0 // X_QUANT[a] * X_QUANT[a]
            return tile("x_bf%d_%d" % (a, g0), [P, PACK * X_QUANT[a]], BF16), c0 - g0

        def x_codes(a, j0):
            return tile("x_codes%d_%d" % (a, j0 // BANK * BANK), [P, BANK], U32)

        def wm_codes(a, c0):
            return tile("wm_codes%d_%d" % (a, c0 // CHUNK * CHUNK), [P, CHUNK], U32)

        def x_cast(engine, a, c0, t0, t1):
            staged, at = x_bf(a, c0)
            dst = staged[:, PACK * at : PACK * (at + CHUNK)].rearrange("p (c i t) -> p c t i", i=4, t=PACK)
            src = picked(a)[:, t0:t1, c0 : c0 + CHUNK].rearrange("p t (c i) -> p c t i", i=4)
            copy_on(engine, dst[:, :, t0:t1], src)

        def x_quant(a, c0):
            width = X_QUANT[a]
            quantize(x_codes(a, c0)[:, c0 % BANK : c0 % BANK + width], x_scales[:, a, c0 : c0 + width], x_bf(a, c0)[0][:])

        def wm_cast(engine, a, c0):
            staged = tile("wm_bf%d_%d" % (a, c0), [P, PACK * CHUNK], BF16)
            copy_on(engine, staged[:].rearrange("p (c i t) -> p c t i", i=4, t=PACK), wm_raw[(a, c0)].rearrange("p t (c i) -> p c t i", i=4))

        def wm_quant(a, c0):
            quantize(wm_codes(a, c0)[:], wm_scales[:, a, c0 : c0 + CHUNK], made["wm_bf%d_%d" % (a, c0)][:])

        def w1_cast(engine, a, t0):
            copy_on(
                engine,
                tile("w1_bf%d" % a, [P, PACK * H], BF16)[:].rearrange("p (t m i) -> p m i t", t=PACK, i=PACK)[:, :, :, t0 : t0 + 2],
                made["w1_raw%d" % a][:].rearrange("p i (m t) -> p m i t", t=PACK)[:, :, :, t0 : t0 + 2],
            )

        def w1_quant(a):
            quantize(tile("w1_codes%d" % a, [P, H], U32)[:], w1_scales[:, a, :], made["w1_bf%d" % a][:])

        def mx(acc, wc, ws, xc, xs, start, stop, wdt=FP8X4):
            nc.tensor.matmul_mx(
                out=acc, lhsT=wc.bitcast(wdt), lhsT_scale=ws, rhs=xc.bitcast(FP8X4), rhs_scale=xs, start=start, stop=stop
            )

        def hidden(j0):
            c0 = j0 % BANK
            acc = psum.tile([P, PACK, H_CHUNK], F32, name="acc")
            for t in range(PACK):
                ms = slice(t * P, (t + 1) * P)
                for a in range(PASSES):
                    mx(acc[:, t, :], made["w1_codes%d" % a][:, ms], w1_scales[:, a, ms], x_codes(a, j0)[:, c0 : c0 + H_CHUNK],
                       x_scales[:, a, j0 : j0 + H_CHUNK], a == 0, a == PASSES - 1)
            th = tile("th%d" % (j0 - c0), [P, BANK, PACK], F32)
            nc.scalar.activation(out=th[:, c0 : c0 + H_CHUNK, :], in_=acc[:].rearrange("p t j -> p j t"), func=ACT.Tanh)

        def gained(j0, width):
            c0 = j0 % BANK
            h_bf = tile("h_bf%d" % (j0 - c0), [P, PACK * BANK], BF16)
            nc.vector.tensor_tensor(
                h_bf[:, PACK * c0 : PACK * (c0 + width)].rearrange("p (j t) -> p j t", t=PACK),
                made["th%d" % (j0 - c0)][:, c0 : c0 + width, :],
                gain_sb[:].unsqueeze(1).to_broadcast([P, width, PACK]),
                MULT,
            )

        def h_quant(j0, width):
            c0 = j0 % BANK
            quantize(h_codes[:, j0 : j0 + width], h_scales[:, j0 : j0 + width],
                     made["h_bf%d" % (j0 - c0)][:, PACK * c0 : PACK * (c0 + width)])

        def mask_of(n, j0, width):
            ns = slice(n * P, (n + 1) * P)
            js = slice(j0, j0 + width)
            acc = psum.tile([P, BANK], F32, name="acc")
            for a in range(PASSES):
                mx(acc[:, 0:width], wm_codes(a, n * P)[:, n % 2 * P : (n % 2 + 1) * P], wm_scales[:, a, ns],
                   x_codes(a, j0)[:, j0 % BANK : j0 % BANK + width], x_scales[:, a, js], a == 0, a == PASSES - 1)
            mask = tile("mask%d" % (n // 2), [P, 2, S], F32)[:, n % 2, js]
            nc.scalar.activation(out=mask, in_=acc[:, 0:width], func=ACT.Sigmoid, bias=bm_sb[:, n : n + 1])

        def finish(n, j0, width):
            ns = slice(n * P, (n + 1) * P)
            js = slice(j0, j0 + width)
            acc = psum.tile([P, BANK], F32, name="acc")
            mx(acc[:, 0:width], w2_codes[:, 2 * n * P : 2 * (n + 1) * P], w2_plane[:, ns], h_codes[:, js], h_scales[:, js],
               True, True, FP4X4)
            mask = made["mask%d" % (n // 2)][:, n % 2, js]
            nc.vector.tensor_tensor(mask, acc[:, 0:width], mask, MULT)
            nc.sync.dma_start(out=out[ns, js], in_=mask)

        nc.gpsimd.memset(w2_plane[:].bitcast(I32), 0)
        nc.gpsimd.memset(warm[:, 0:8], 0.0)
        nc.scalar.activation(out=warm[:, 8:16], in_=warm[:, 0:8], func=ACT.Sigmoid)
        load_plane(0, 0)
        nc.sync.dma_start(offsets[:], offs)
        load_wgt(0, 512)
        load_wgt(512, 1024)
        load_plane(0, 1)
        load_plane(0, 2)
        load_plane(0, 3)
        load_plane(1, 0)
        load_plane(1, 1)
        load_plane(1, 2)
        load_w1(0)
        load_plane(1, 3)
        load_w1(1)
        load_wm(1, 0, 512)
        load_wm(0, 0, 512)
        load_bm()
        load_wm(0, 512, 768)
        load_gain()
        load_wm(1, 512, 768)
        load_w2_scales(0)
        load_w2_scales(1)
        load_w2_scales(2)
        load_w2_scales(3)
        load_w2_codes()
        gather(0, 0, 0, 512)
        gather(0, 0, 512, 1024)
        gather(0, 1, 0, 512)
        gather(0, 1, 512, 1024)
        gather(0, 2, 0, 512)
        gather(0, 2, 512, 1024)
        gather(0, 3, 0, 512)
        gather(0, 3, 512, 1024)
        gather(1, 0, 0, 512)
        gather(1, 0, 512, 1024)
        gather(1, 1, 0, 512)
        gather(1, 1, 512, 1024)
        gather(1, 2, 0, 512)
        gather(1, 2, 512, 1024)
        gather(1, 3, 0, 256)
        gather(1, 3, 256, 512)
        gather(1, 3, 512, 768)
        gather(1, 3, 768, 1024)
        x_cast("S", 0, 0, 0, 4)
        x_cast("S", 0, 256, 0, 4)
        x_quant(0, 0)
        x_cast("S", 0, 512, 0, 4)
        x_cast("S", 0, 768, 0, 4)
        x_quant(0, 512)
        w1_cast("S", 0, 0)
        w1_cast("S", 0, 2)
        w1_quant(0)
        x_cast("S", 1, 0, 0, 4)
        x_cast("V", 1, 256, 0, 4)
        x_quant(1, 0)
        w1_cast("S", 1, 0)
        w1_cast("S", 1, 2)
        w1_quant(1)
        x_cast("V", 1, 512, 0, 4)
        x_cast("V", 1, 768, 0, 4)
        x_quant(1, 512)
        wm_cast("V", 0, 0)
        wm_quant(0, 0)
        wm_cast("S", 1, 0)
        wm_quant(1, 0)
        wm_cast("V", 0, 256)
        wm_quant(0, 256)
        wm_cast("S", 1, 256)
        wm_quant(1, 256)
        hidden(0)
        gained(0, 128)
        hidden(128)
        gained(128, 128)
        h_quant(0, 256)
        hidden(256)
        gained(256, 128)
        hidden(384)
        gained(384, 128)
        h_quant(256, 256)
        hidden(512)
        gained(512, 128)
        hidden(640)
        gained(640, 128)
        h_quant(512, 256)
        hidden(768)
        gained(768, 128)
        hidden(896)
        gained(896, 128)
        h_quant(768, 256)
        mask_of(0, 0, 512)
        mask_of(1, 0, 512)
        finish(0, 0, 512)
        mask_of(2, 0, 512)
        finish(1, 0, 512)
        mask_of(3, 0, 512)
        finish(2, 0, 512)
        mask_of(0, 512, 512)
        finish(3, 0, 512)
        wm_cast("S", 0, 512)
        wm_quant(0, 512)
        wm_cast("S", 1, 512)
        wm_quant(1, 512)
        mask_of(1, 512, 512)
        finish(0, 512, 512)
        mask_of(2, 512, 512)
        finish(1, 512, 512)
        mask_of(3, 512, 512)
        finish(2, 512, 512)
        mask_of(4, 0, 512)
        finish(3, 512, 512)
        mask_of(5, 0, 512)
        finish(4, 0, 512)
        mask_of(4, 512, 512)
        finish(5, 0, 512)
        mask_of(5, 512, 512)
        finish(4, 512, 512)
        finish(5, 512, 512)
